import numpy as np
import ml_dtypes


def mxq(x, axis, fmt="e4m3"):
    dtype, down = {"e4m3": (ml_dtypes.float8_e4m3fn, 7), "e5m2": (ml_dtypes.float8_e5m2, 14)}[fmt]
    v = np.moveaxis(np.asarray(x, np.float32).astype(ml_dtypes.bfloat16).astype(np.float64), axis, -1)
    blocks = v.reshape(v.shape[:-1] + (-1, 32))
    amax = np.abs(blocks).max(-1, keepdims=True)
    byte = np.maximum(np.where(amax > 0, np.frexp(amax)[1] - 1 + 127, 0) - down, 1)
    scale = np.exp2(byte - 127.0)
    codes = (blocks / scale).astype(np.float32).astype(dtype).astype(np.float64)
    return np.moveaxis((codes * scale).reshape(v.shape), -1, axis)


WIDE = False


def mx_kscale(k):
    if not WIDE:
        return np.ones(k)
    levels = np.array([10, -10, 5, -5, 0])
    if k % 512:
        return np.exp2(np.random.permutation(np.resize(levels, k // 32))).repeat(32)
    a = np.empty((k // 512, 16))
    for p in range(k // 512):
        a[p, :8] = np.random.permutation(np.resize(levels, 8))
        for g in range(8):
            far = levels[np.abs(levels - a[p, g]) >= 10]
            a[p, g + 8] = far[np.random.randint(len(far))]
    return np.exp2(a.ravel()).repeat(32)


def f64(x):
    return np.asarray(x).astype(np.float64)


def striped(idx):
    return np.tile(idx.reshape(-1, 16).T, (8, 1)).astype(np.uint16)


def unstriped(offs):
    return offs[:16].T.reshape(-1).astype(np.int64)


def striped8(idx):
    return np.concatenate([x.reshape(-1, 16).T for x in idx]).astype(np.uint16)


def runs(offs, k):
    lists = np.stack([offs[16 * r : 16 * r + 16].T.reshape(-1) for r in range(8)]).astype(np.int64)
    return lists[np.arange(k) % 512 // 64]


def pack_weight(w):
    k, n = w.shape
    w = f64(np.asarray(w, np.float32).astype(ml_dtypes.bfloat16)).reshape(k // 32, 32, n)
    amax = np.abs(w).max(1)
    byte = np.clip(np.where(amax > 0, np.frexp(amax)[1] - 1 + 127 - 7, 1), 1, 254)
    scaled = (w * np.exp2(127.0 - byte)[:, None, :]).reshape(k, n).astype(np.float32)
    words = np.ascontiguousarray(scaled.reshape(k // 512, 128, 4, n).transpose(0, 1, 3, 2)).astype(ml_dtypes.float8_e4m3fn).view(np.uint8)
    return words, np.ascontiguousarray(byte.astype(np.uint8).reshape(k // 512, 16, n))


def unpack_weight(words, scales):
    g, p, n, _ = words.shape
    vals = np.ascontiguousarray(words).view(ml_dtypes.float8_e4m3fn).astype(np.float64) * np.repeat(np.exp2(scales.astype(np.float64) - 127.0), 8, axis=1)[..., None]
    return vals.transpose(0, 1, 3, 2).reshape(g * 512, n)


def sigmoid(v):
    return 1.0 / (1.0 + np.exp(-np.maximum(v, -700.0)))


K, T, S, N, H = 512, 2048, 512, 512, 512


def setup_inputs():
    n = np.random.standard_normal
    s = mx_kscale(K)[:, None]
    u = mx_kscale(H)
    packed_xT = pack_weight(n((K, T)) * s)
    return {
        "x_words": packed_xT[0],
        "x_scales": packed_xT[1],
        "w1": (n((K, H)) / np.sqrt(K) / s).astype(np.float32),
        "gn": (np.random.uniform(0.5, 1.5, (H, 1)) * u[:, None]).astype(np.float32),
        "w2": (n((H, N)) / np.sqrt(H) / u[:, None]).astype(np.float32),
        "offs": striped(np.random.permutation(T)[:S]),
        "n1": striped8(np.stack([np.random.permutation(S) for _ in range(8)])),
        "n2": striped8(np.stack([np.random.permutation(S) for _ in range(8)])),
        "n3": striped8(np.stack([np.random.permutation(S) for _ in range(8)])),
    }


def reference(x_words, x_scales, w1, gn, w2, offs, n1, n2, n3):
    xq = unpack_weight(x_words, x_scales)[:, unstriped(offs)]
    y = mxq(f64(w1), 0, "e4m3").T @ xq
    z = f64(gn) * (np.abs(y[np.arange(H)[:, None], runs(n1, H)] + y[np.arange(H)[:, None], runs(n2, H)] - y))
    h = mxq(f64(w2), 0, "e4m3").T @ mxq(z, 0, "e4m3")
    a = h[np.arange(N)[:, None], runs(n3, N)]
    return sigmoid(a) * (h - a)

@@ -1,0 +1,236 @@
+from contextlib import ExitStack
+
+import concourse.mybir as mybir
+
+F32 = mybir.dt.float32
+BF16 = mybir.dt.bfloat16
+I32 = mybir.dt.int32
+U32 = mybir.dt.uint32
+U16 = mybir.dt.uint16
+U8 = mybir.dt.uint8
+FP8X4 = mybir.dt.float8_e4m3fn_x4
+ACT = mybir.ActivationFunctionType
+ALU = mybir.AluOpType
+
+P = 128
+PACK = 4
+T = 2048
+S = 512
+HALF = 256
+QUARTER = 128
+FLOPS = 2 * 2 * 512 * 512 * 512
+CHUNKS = [(0, 256), (256, 128), (384, 128)]
+
+
+def tile_picked_absgate_none_p_kernel(
+    tc, x_words, x_scales, w1, gn, w2, offs, n1, n2, n3, out
+):
+    nc = tc.nc
+    with ExitStack() as ctx:
+        keep = ctx.enter_context(tc.tile_pool(name="keep", bufs=1))
+        psum = ctx.enter_context(tc.psum_pool(name="psum", bufs=1))
+
+        def sb(name, shape, dtype, tag=""):
+            return keep.tile(shape, dtype, name=name, tag=tag or name, align_bytes=64)
+
+        def entries(lst, start, width):
+            return lst[:, start // 16 : (start + width) // 16]
+
+        offs_sb = keep.tile([P, S // 16], U16, name="offs_sb")
+        n1_sb = keep.tile([P, S // 16], U16, name="n1_sb")
+        n2_sb = keep.tile([P, S // 16], U16, name="n2_sb")
+        n3_sb = keep.tile([P, S // 16], U16, name="n3_sb")
+
+        xs_all = sb("xs_all", [P, T], U8)
+        nc.vector.memset(xs_all[:].bitcast(I32), 0)
+        for q in range(4):
+            nc.scalar.dma_start(
+                out=xs_all[32 * q : 32 * q + 4, :].bitcast(I32), in_=x_scales[0][4 * q : 4 * q + 4, :].bitcast(I32)
+            )
+        warm = sb("warm", [P, 8], F32)
+        nc.vector.memset(warm[:, 0:1], 0.0)
+        nc.scalar.activation(warm[:, 4:5], warm[:, 0:1], ACT.Sigmoid)
+
+        nc.sync.dma_start(offs_sb[:], offs)
+        nc.sync.dma_start(n1_sb[:], n1)
+        nc.sync.dma_start(n2_sb[:], n2)
+        w1_rows = w1.rearrange("(p j) c -> p j c", j=PACK)
+        w1_raw = []
+        for a in range(2):
+            raw = sb("w1_raw%d" % a, [P, PACK, HALF], F32, tag="chain_a" if a == 0 else "")
+            nc.sync.dma_start(out=raw[:], in_=w1_rows[:, :, a * HALF : (a + 1) * HALF])
+            w1_raw.append(raw)
+        xw_all = sb("xw_all", [P, T], I32)
+        nc.sync.dma_start(out=xw_all[:], in_=x_words[0].rearrange("p n t -> p (n t)").bitcast(I32))
+        nc.sync.dma_start(n3_sb[:], n3)
+        gain = sb("gain", [P, PACK], F32)
+        nc.gpsimd.dma_start(out=gain[:], in_=gn.rearrange("(p j) o -> p (j o)", j=PACK))
+
+        g1 = sb("g1", [P, PACK * S], BF16)
+        g1_v = g1[:].rearrange("p (t m j) -> p m t j", t=PACK, j=PACK)
+        for a in range(2):
+            nc.vector.tensor_copy(g1_v[:, 64 * a : 64 * (a + 1)], w1_raw[a][:].rearrange("p j (m t) -> p m t j", t=PACK))
+        w2_raw = sb("w2_raw", [P, PACK, S], F32, tag="chain_a")
+        nc.sync.dma_start(out=w2_raw[:], in_=w2.rearrange("(p j) c -> p j c", j=PACK))
+        xs = sb("xs", [P, S], U8)
+        xw = sb("xw", [P, S], U32)
+        nc.vector.tensor_copy(xs[:], xs_all[:].indirect(offs_sb[:]))
+        w1c = sb("w1c", [P, S], U32)
+        w1s = sb("w1s", [P, S], U8)
+        nc.vector.quantize_mx(out=w1c[:].bitcast(FP8X4), scales=w1s[:], in_=g1[:])
+        for a in range(2):
+            nc.vector.tensor_copy(
+                xw[:, a * HALF : (a + 1) * HALF], xw_all[:].bitcast(U32).indirect(entries(offs_sb, a * HALF, HALF))
+            )
+
+        sign = sb("sign", [P, PACK], F32)
+        nc.scalar.activation(sign[:], gain[:], ACT.Sign)
+
+        def product(acc, wc, ws, t, rc, rs):
+            nc.tensor.matmul_mx(
+                out=acc,
+                lhsT=wc[:, t * P : (t + 1) * P].bitcast(FP8X4),
+                lhsT_scale=ws[:, t * P : (t + 1) * P],
+                rhs=rc.bitcast(FP8X4),
+                rhs_scale=rs,
+                start=True,
+                stop=True,
+            )
+
+        y_win = [sb("y_win%d" % t, [P, S], F32) for t in range(PACK)]
+        y_lo = [sb("y_lo%d" % t, [P, HALF], F32) for t in range(PACK)]
+        y_hi = [sb("y_hi%d" % t, [P, HALF], F32) for t in range(PACK)]
+        acc_a = psum.tile([P, HALF], F32, name="acc_a", tag="b0")
+        acc_b = psum.tile([P, HALF], F32, name="acc_b", tag="b4")
+        product(acc_a[:], w1c, w1s, 0, xw[:, 0:HALF], xs[:, 0:HALF])
+        product(acc_b[:], w1c, w1s, 0, xw[:, HALF:S], xs[:, HALF:S])
+        accs = [None]
+        for t in range(1, PACK):
+            acc = psum.tile([P, S], F32, name="acc_y%d" % t, tag="b%d" % t)
+            product(acc[:], w1c, w1s, t, xw[:], xs[:])
+            accs.append(acc)
+        nc.scalar.activation(y_win[0][:, 0:HALF], acc_a[:], ACT.Copy, scale=gain[:, 0:1])
+        nc.vector.tensor_scalar(y_win[0][:, HALF:S], acc_b[:], gain[:, 0:1], None, ALU.mult)
+        nc.scalar.activation(y_lo[0][:], acc_a[:], ACT.Copy, scale=gain[:, 0:1])
+        nc.sync.dma_start(out=y_hi[0][:], in_=y_win[0][:, HALF:S])
+        for t in range(1, PACK):
+            nc.scalar.activation(y_win[t][:], accs[t][:], ACT.Copy, scale=gain[:, t : t + 1])
+            nc.scalar.activation(y_lo[t][:], accs[t][:, 0:HALF], ACT.Copy, scale=gain[:, t : t + 1])
+            nc.sync.dma_start(out=y_hi[t][:], in_=y_win[t][:, HALF:S])
+
+        def y_plain(t, start, width):
+            if start < HALF:
+                return y_lo[t][:, start : start + width]
+            return y_hi[t][:, start - HALF : start - HALF + width]
+
+        def first(c, t, tag=""):
+            start, width = CHUNKS[c]
+            part = sb("part%d_%d" % (c, t), [P, width], F32, tag=tag)
+            nc.vector.tensor_tensor(
+                part[:], y_win[t][:].indirect(entries(n1_sb, start, width)), y_plain(t, start, width), ALU.subtract
+            )
+            return part
+
+        def second(c, t, part, d):
+            start, width = CHUNKS[c]
+            nc.vector.tensor_tensor(
+                d[:, t * width : (t + 1) * width], y_win[t][:].indirect(entries(n2_sb, start, width)), part[:], ALU.add
+            )
+
+        def gathers(c, tags):
+            d = sb("d%d" % c, [P, PACK * CHUNKS[c][1]], F32)
+            parts = [first(c, 0, tags[0])]
+            for t in range(1, PACK):
+                parts.append(first(c, t, tags[t]))
+                second(c, t - 1, parts[t - 1], d)
+            second(c, PACK - 1, parts[PACK - 1], d)
+            return d
+
+        def magnitude(c, d, tag):
+            zb = sb("zb%d" % c, [P, PACK * CHUNKS[c][1]], BF16, tag=tag)
+            nc.scalar.activation(
+                zb[:].rearrange("p (c i t) -> p c t i", i=4, t=PACK),
+                d[:].rearrange("p (t c i) -> p c t i", i=4, t=PACK),
+                ACT.Abs,
+            )
+            return zb
+
+        def quantise(c, zb):
+            width = CHUNKS[c][1]
+            zc = sb("zc%d" % c, [P, width], U32)
+            zs = sb("zs%d" % c, [P, width], U8)
+            nc.vector.quantize_mx(out=zc[:].bitcast(FP8X4), scales=zs[:], in_=zb[:])
+            return zc, zs
+
+        d0 = gathers(0, ["", "", "", ""])
+        pairs = sb("pairs", [P, PACK * S], BF16)
+        pairs_v = pairs[:].rearrange("p (u c e) -> p u c e", u=2, e=2)
+        for j in range(PACK):
+            nc.scalar.activation(pairs_v[:, j // 2, :, j % 2], w2_raw[:, j, :], ACT.Copy, scale=sign[:, j : j + 1])
+        zb0 = magnitude(0, d0, "chain_a")
+        d1 = gathers(1, ["", "", "", ""])
+        zb1 = magnitude(1, d1, "chain_c")
+        g2 = sb("g2", [P, PACK * S], BF16, tag="chain_b")
+        nc.vector.tensor_copy(
+            g2[:].bitcast(F32).rearrange("p (t m u) -> p m t u", t=PACK, u=2),
+            pairs[:].bitcast(F32).rearrange("p (u m t) -> p m t u", t=PACK, u=2),
+        )
+        zq0 = quantise(0, zb0)
+        w2c = sb("w2c", [P, S], U32)
+        w2s = sb("w2s", [P, S], U8)
+        nc.vector.quantize_mx(out=w2c[:].bitcast(FP8X4), scales=w2s[:], in_=g2[:])
+
+        h_win = [sb("h_win%d" % t, [P, S], F32) for t in range(PACK)]
+        h_half = [[sb("h_half%d_%d" % (a, t), [P, HALF], F32) for t in range(PACK)] for a in range(2)]
+
+        banks0 = [psum.tile([P, 2, HALF], F32, name="acc_h0_%d" % a, tag="b%d" % (5 + a)) for a in range(2)]
+        for t in range(PACK):
+            product(banks0[t // 2][:, t % 2, :], w2c, w2s, t, zq0[0][:], zq0[1][:])
+        for t in range(PACK):
+            nc.scalar.copy(h_win[t][:, 0:HALF], banks0[t // 2][:, t % 2, :])
+            nc.sync.dma_start(out=h_half[0][t][:], in_=h_win[t][:, 0:HALF])
+
+        d2 = sb("d2", [P, PACK * QUARTER], F32)
+        p0 = first(2, 0, "chain_b")
+        p1 = first(2, 1, "chain_a")
+        second(2, 0, p0, d2)
+        second(2, 1, p1, d2)
+        zq1 = quantise(1, zb1)
+        bank1 = psum.tile([P, PACK, QUARTER], F32, name="acc_h1", tag="b7")
+        for t in range(PACK):
+            product(bank1[:, t, :], w2c, w2s, t, zq1[0][:], zq1[1][:])
+        for t in range(PACK):
+            nc.scalar.copy(h_win[t][:, HALF : HALF + QUARTER], bank1[:, t, :])
+        p2 = first(2, 2, "chain_c")
+        p3 = first(2, 3, "")
+        second(2, 2, p2, d2)
+        second(2, 3, p3, d2)
+        zb2 = magnitude(2, d2, "")
+        zq2 = quantise(2, zb2)
+        for t in range(PACK):
+            acc = psum.tile([P, QUARTER], F32, name="acc_h2_%d" % t, tag="b%d" % t)
+            product(acc[:], w2c, w2s, t, zq2[0][:], zq2[1][:])
+            nc.scalar.copy(h_win[t][:, HALF + QUARTER : S], acc[:])
+            nc.sync.dma_start(out=h_half[1][t][:], in_=h_win[t][:, HALF:S])
+
+        out_rows = out.rearrange("(p t) c -> p t c", t=PACK)
+        units = [(a, t) for a in range(2) for t in range(PACK)]
+
+        def look_up(a, t):
+            places = entries(n3_sb, a * HALF, HALF)
+            diff = sb("diff%d_%d" % (a, t), [P, HALF], F32)
+            gate = sb("gate%d_%d" % (a, t), [P, HALF], F32)
+            nc.vector.tensor_tensor(diff[:], h_win[t][:].indirect(places), h_half[a][t][:], ALU.subtract)
+            nc.scalar.activation(gate[:], h_win[t][:].indirect(places), ACT.Sigmoid)
+            return diff, gate
+
+        def finish(a, t, diff, gate):
+            res = sb("res%d_%d" % (a, t), [P, HALF], F32)
+            nc.vector.scalar_tensor_tensor(res[:], diff[:], -1.0, gate[:], ALU.mult, ALU.mult)
+            nc.sync.dma_start(out=out_rows[:, t, a * HALF : (a + 1) * HALF], in_=res[:])
+
+        looked = [look_up(*units[0])]
+        for k in range(1, len(units)):
+            looked.append(look_up(*units[k]))
+            finish(*units[k - 1], *looked[k - 1])
+        finish(*units[-1], *looked[-1])

@@ -19,7 +19,6 @@ S = 512
 HALF = 256
 QUARTER = 128
 FLOPS = 2 * 2 * 512 * 512 * 512
-CHUNKS = [(0, 256), (256, 128), (384, 128)]
 
 
 def tile_picked_absgate_none_p_kernel(
@@ -98,139 +97,153 @@ def tile_picked_absgate_none_p_kernel(
             )
 
         y_win = [sb("y_win%d" % t, [P, S], F32) for t in range(PACK)]
-        y_lo = [sb("y_lo%d" % t, [P, HALF], F32) for t in range(PACK)]
+        d0 = sb("d0", [P, PACK * HALF], F32)
+        y_lo_even = [sb("y_lo%d" % t, [P, HALF], F32) for t in (0, 2)]
+        y_lo = [y_lo_even[0][:], d0[:, 0:HALF], y_lo_even[1][:], d0[:, 2 * HALF : 3 * HALF]]
         y_hi = [sb("y_hi%d" % t, [P, HALF], F32) for t in range(PACK)]
-        acc_a = psum.tile([P, HALF], F32, name="acc_a", tag="b0")
-        acc_b = psum.tile([P, HALF], F32, name="acc_b", tag="b4")
-        product(acc_a[:], w1c, w1s, 0, xw[:, 0:HALF], xs[:, 0:HALF])
-        product(acc_b[:], w1c, w1s, 0, xw[:, HALF:S], xs[:, HALF:S])
-        accs = [None]
-        for t in range(1, PACK):
-            acc = psum.tile([P, S], F32, name="acc_y%d" % t, tag="b%d" % t)
-            product(acc[:], w1c, w1s, t, xw[:], xs[:])
-            accs.append(acc)
-        nc.scalar.activation(y_win[0][:, 0:HALF], acc_a[:], ACT.Copy, scale=gain[:, 0:1])
-        nc.vector.tensor_scalar(y_win[0][:, HALF:S], acc_b[:], gain[:, 0:1], None, ALU.mult)
-        nc.scalar.activation(y_lo[0][:], acc_a[:], ACT.Copy, scale=gain[:, 0:1])
-        nc.sync.dma_start(out=y_hi[0][:], in_=y_win[0][:, HALF:S])
-        for t in range(1, PACK):
-            nc.scalar.activation(y_win[t][:], accs[t][:], ACT.Copy, scale=gain[:, t : t + 1])
-            nc.scalar.activation(y_lo[t][:], accs[t][:, 0:HALF], ACT.Copy, scale=gain[:, t : t + 1])
+        lo_acc = [psum.tile([P, HALF], F32, name="acc_lo%d" % t, tag="b%d" % t) for t in range(2)]
+        hi_acc = [psum.tile([P, HALF], F32, name="acc_hi%d" % t, tag="b%d" % (4 + t)) for t in range(2)]
+        full_acc = [psum.tile([P, S], F32, name="acc_y%d" % t, tag="b%d" % t) for t in (2, 3)]
+        for t in range(2):
+            product(lo_acc[t][:], w1c, w1s, t, xw[:, 0:HALF], xs[:, 0:HALF])
+        for t in range(2):
+            product(hi_acc[t][:], w1c, w1s, t, xw[:, HALF:S], xs[:, HALF:S])
+        for t in (2, 3):
+            product(full_acc[t - 2][:], w1c, w1s, t, xw[:], xs[:])
+
+        def scaled(dst, acc, t):
+            nc.scalar.activation(dst, acc, ACT.Copy, scale=gain[:, t : t + 1])
+
+        for t in range(2):
+            scaled(y_win[t][:, 0:HALF], lo_acc[t][:], t)
+            scaled(y_lo[t], lo_acc[t][:], t)
+        nc.vector.tensor_scalar(y_win[0][:, HALF:S], hi_acc[0][:], gain[:, 0:1], None, ALU.mult)
+        scaled(y_win[1][:, HALF:S], hi_acc[1][:], 1)
+        for t in (2, 3):
+            scaled(y_win[t][:], full_acc[t - 2][:], t)
+            scaled(y_lo[t], full_acc[t - 2][:, 0:HALF], t)
+        for t in range(PACK):
             nc.sync.dma_start(out=y_hi[t][:], in_=y_win[t][:, HALF:S])
 
-        def y_plain(t, start, width):
-            if start < HALF:
-                return y_lo[t][:, start : start + width]
-            return y_hi[t][:, start - HALF : start - HALF + width]
-
-        def first(c, t, tag=""):
-            start, width = CHUNKS[c]
-            part = sb("part%d_%d" % (c, t), [P, width], F32, tag=tag)
-            nc.vector.tensor_tensor(
-                part[:], y_win[t][:].indirect(entries(n1_sb, start, width)), y_plain(t, start, width), ALU.subtract
-            )
+        def first(t, start, plain):
+            part = sb("part%d_%d" % (start, t), [P, HALF], F32)
+            nc.vector.tensor_tensor(part[:], y_win[t][:].indirect(entries(n1_sb, start, HALF)), plain, ALU.subtract)
             return part
 
-        def second(c, t, part, d):
-            start, width = CHUNKS[c]
+        def second(t, start, width, part, d):
             nc.vector.tensor_tensor(
-                d[:, t * width : (t + 1) * width], y_win[t][:].indirect(entries(n2_sb, start, width)), part[:], ALU.add
+                d[:, t * width : (t + 1) * width], y_win[t][:].indirect(entries(n2_sb, start, width)), part, ALU.add
             )
 
-        def gathers(c, tags):
-            d = sb("d%d" % c, [P, PACK * CHUNKS[c][1]], F32)
-            parts = [first(c, 0, tags[0])]
-            for t in range(1, PACK):
-                parts.append(first(c, t, tags[t]))
-                second(c, t - 1, parts[t - 1], d)
-            second(c, PACK - 1, parts[PACK - 1], d)
-            return d
-
-        def magnitude(c, d, tag):
-            zb = sb("zb%d" % c, [P, PACK * CHUNKS[c][1]], BF16, tag=tag)
+        def magnitude(zb, d):
             nc.scalar.activation(
                 zb[:].rearrange("p (c i t) -> p c t i", i=4, t=PACK),
                 d[:].rearrange("p (t c i) -> p c t i", i=4, t=PACK),
                 ACT.Abs,
             )
-            return zb
 
-        def quantise(c, zb):
-            width = CHUNKS[c][1]
-            zc = sb("zc%d" % c, [P, width], U32)
-            zs = sb("zs%d" % c, [P, width], U8)
+        def quantise(name, zb, width):
+            zc = sb("zc" + name, [P, width], U32)
+            zs = sb("zs" + name, [P, width], U8)
             nc.vector.quantize_mx(out=zc[:].bitcast(FP8X4), scales=zs[:], in_=zb[:])
             return zc, zs
 
-        d0 = gathers(0, ["", "", "", ""])
+        for pair in ((0, 1), (2, 3)):
+            parts = [first(t, 0, y_lo[t]) for t in pair]
+            for t, part in zip(pair, parts):
+                second(t, 0, HALF, part[:], d0)
         pairs = sb("pairs", [P, PACK * S], BF16)
         pairs_v = pairs[:].rearrange("p (u c e) -> p u c e", u=2, e=2)
         for j in range(PACK):
             nc.scalar.activation(pairs_v[:, j // 2, :, j % 2], w2_raw[:, j, :], ACT.Copy, scale=sign[:, j : j + 1])
-        zb0 = magnitude(0, d0, "chain_a")
-        d1 = gathers(1, ["", "", "", ""])
-        zb1 = magnitude(1, d1, "chain_c")
+        zb0 = sb("zb0", [P, PACK * HALF], BF16, tag="chain_a")
+        magnitude(zb0, d0)
+        hi_parts = [first(t, HALF, y_hi[t][:]) for t in range(PACK)]
         g2 = sb("g2", [P, PACK * S], BF16, tag="chain_b")
-        nc.vector.tensor_copy(
+        nc.scalar.copy(
             g2[:].bitcast(F32).rearrange("p (t m u) -> p m t u", t=PACK, u=2),
             pairs[:].bitcast(F32).rearrange("p (u m t) -> p m t u", t=PACK, u=2),
         )
-        zq0 = quantise(0, zb0)
+        zq0 = quantise("0", zb0, HALF)
+        d1 = sb("d1", [P, PACK * QUARTER], F32, tag="chain_a")
+        for t in range(PACK):
+            second(t, HALF, QUARTER, hi_parts[t][:, 0:QUARTER], d1)
+        zb1 = sb("zb1", [P, PACK * QUARTER], BF16)
+        magnitude(zb1, d1)
         w2c = sb("w2c", [P, S], U32)
         w2s = sb("w2s", [P, S], U8)
         nc.vector.quantize_mx(out=w2c[:].bitcast(FP8X4), scales=w2s[:], in_=g2[:])
 
         h_win = [sb("h_win%d" % t, [P, S], F32) for t in range(PACK)]
         h_half = [[sb("h_half%d_%d" % (a, t), [P, HALF], F32) for t in range(PACK)] for a in range(2)]
+        lo_h = [psum.tile([P, HALF], F32, name="acc_h0_%d" % t, tag="b%d" % t) for t in range(PACK)]
+        for t in range(PACK):
+            product(lo_h[t][:], w2c, w2s, t, zq0[0][:], zq0[1][:])
 
-        banks0 = [psum.tile([P, 2, HALF], F32, name="acc_h0_%d" % a, tag="b%d" % (5 + a)) for a in range(2)]
-        for t in range(PACK):
-            product(banks0[t // 2][:, t % 2, :], w2c, w2s, t, zq0[0][:], zq0[1][:])
-        for t in range(PACK):
-            nc.scalar.copy(h_win[t][:, 0:HALF], banks0[t // 2][:, t % 2, :])
-            nc.sync.dma_start(out=h_half[0][t][:], in_=h_win[t][:, 0:HALF])
+        def keep_half(a, t, acc, copy):
+            copy(h_win[t][:, a * HALF : (a + 1) * HALF], acc)
+            nc.sync.dma_start(out=h_half[a][t][:], in_=h_win[t][:, a * HALF : (a + 1) * HALF])
 
-        d2 = sb("d2", [P, PACK * QUARTER], F32)
-        p0 = first(2, 0, "chain_b")
-        p1 = first(2, 1, "chain_a")
-        second(2, 0, p0, d2)
-        second(2, 1, p1, d2)
-        zq1 = quantise(1, zb1)
-        bank1 = psum.tile([P, PACK, QUARTER], F32, name="acc_h1", tag="b7")
+        for t in range(2):
+            keep_half(0, t, lo_h[t][:], nc.scalar.copy)
+        d2 = sb("d2", [P, PACK * QUARTER], F32, tag="chain_b")
+        zb2 = sb("zb2", [P, PACK * QUARTER], BF16)
         for t in range(PACK):
-            product(bank1[:, t, :], w2c, w2s, t, zq1[0][:], zq1[1][:])
+            second(t, HALF + QUARTER, QUARTER, hi_parts[t][:, QUARTER:HALF], d2)
+            if t % 2 == 1:
+                nc.scalar.activation(
+                    zb2[:].rearrange("p (c i u e) -> p u c e i", i=4, u=2, e=2)[:, t // 2],
+                    d2[:].rearrange("p (u e c i) -> p u c e i", i=4, u=2, e=2)[:, t // 2],
+                    ACT.Abs,
+                )
+        zq1 = quantise("1", zb1, QUARTER)
+        hi_h = [psum.tile([P, 2, QUARTER], F32, name="acc_h1_%d" % t, tag="b%d" % (4 + t)) for t in range(PACK)]
         for t in range(PACK):
-            nc.scalar.copy(h_win[t][:, HALF : HALF + QUARTER], bank1[:, t, :])
-        p2 = first(2, 2, "chain_c")
-        p3 = first(2, 3, "")
-        second(2, 2, p2, d2)
-        second(2, 3, p3, d2)
-        zb2 = magnitude(2, d2, "")
-        zq2 = quantise(2, zb2)
+            product(hi_h[t][:, 0, :], w2c, w2s, t, zq1[0][:], zq1[1][:])
+        keep_half(0, 2, lo_h[2][:], nc.vector.tensor_copy)
+        keep_half(0, 3, lo_h[3][:], nc.scalar.copy)
+        zq2 = quantise("2", zb2, QUARTER)
         for t in range(PACK):
-            acc = psum.tile([P, QUARTER], F32, name="acc_h2_%d" % t, tag="b%d" % t)
-            product(acc[:], w2c, w2s, t, zq2[0][:], zq2[1][:])
-            nc.scalar.copy(h_win[t][:, HALF + QUARTER : S], acc[:])
-            nc.sync.dma_start(out=h_half[1][t][:], in_=h_win[t][:, HALF:S])
+            product(hi_h[t][:, 1, :], w2c, w2s, t, zq2[0][:], zq2[1][:])
 
         out_rows = out.rearrange("(p t) c -> p t c", t=PACK)
-        units = [(a, t) for a in range(2) for t in range(PACK)]
+        diff = [sb("diff%d" % a, [P, PACK * HALF], F32) for a in range(2)]
+        gate = [sb("gate%d" % a, [P, PACK * HALF], F32) for a in range(2)]
+        res = [sb("res%d" % a, [P, PACK * HALF], F32) for a in range(2)]
 
-        def look_up(a, t):
-            places = entries(n3_sb, a * HALF, HALF)
-            diff = sb("diff%d_%d" % (a, t), [P, HALF], F32)
-            gate = sb("gate%d_%d" % (a, t), [P, HALF], F32)
-            nc.vector.tensor_tensor(diff[:], h_win[t][:].indirect(places), h_half[a][t][:], ALU.subtract)
-            nc.scalar.activation(gate[:], h_win[t][:].indirect(places), ACT.Sigmoid)
-            return diff, gate
+        def look_up(a, t, lo, width):
+            places = entries(n3_sb, a * HALF + lo, width)
+            cols = slice(t * HALF + lo, t * HALF + lo + width)
+            nc.vector.tensor_tensor(
+                diff[a][:, cols], h_win[t][:].indirect(places), h_half[a][t][:, lo : lo + width], ALU.subtract
+            )
+            nc.scalar.activation(gate[a][:, cols], h_win[t][:].indirect(places), ACT.Sigmoid)
 
-        def finish(a, t, diff, gate):
-            res = sb("res%d_%d" % (a, t), [P, HALF], F32)
-            nc.vector.scalar_tensor_tensor(res[:], diff[:], -1.0, gate[:], ALU.mult, ALU.mult)
-            nc.sync.dma_start(out=out_rows[:, t, a * HALF : (a + 1) * HALF], in_=res[:])
+        def finish(a, t, tiles, lo, width, queue):
+            cols = slice(t * HALF + lo, (t + tiles - 1) * HALF + lo + width)
+            nc.vector.scalar_tensor_tensor(res[a][:, cols], diff[a][:, cols], -1.0, gate[a][:, cols], ALU.mult, ALU.mult)
+            queue.dma_start(
+                out=out_rows[:, t : t + tiles, a * HALF + lo : a * HALF + lo + width],
+                in_=res[a][:, cols].rearrange("p (t c) -> p t c", t=tiles),
+            )
 
-        looked = [look_up(*units[0])]
-        for k in range(1, len(units)):
-            looked.append(look_up(*units[k]))
-            finish(*units[k - 1], *looked[k - 1])
-        finish(*units[-1], *looked[-1])
+        def upper(t):
+            keep_half(1, t, hi_h[t][:].rearrange("p a c -> p (a c)"), nc.scalar.copy)
+
+        upper(0)
+        upper(1)
+        look_up(0, 0, 0, HALF)
+        upper(2)
+        look_up(0, 1, 0, HALF)
+        upper(3)
+        look_up(0, 2, 0, HALF)
+        finish(0, 0, 2, 0, HALF, nc.sync)
+        look_up(0, 3, 0, HALF)
+        look_up(1, 0, 0, HALF)
+        finish(0, 2, 2, 0, HALF, nc.sync)
+        look_up(1, 1, 0, HALF)
+        look_up(1, 2, 0, HALF)
+        finish(1, 0, 2, 0, HALF, nc.sync)
+        look_up(1, 3, 0, HALF)
+        finish(1, 2, 1, 0, HALF, nc.sync)
+        finish(1, 3, 1, 0, HALF, nc.sync)

from contextlib import ExitStack

import concourse.mybir as mybir

F32 = mybir.dt.float32
BF16 = mybir.dt.bfloat16
I32 = mybir.dt.int32
U32 = mybir.dt.uint32
U16 = mybir.dt.uint16
U8 = mybir.dt.uint8
FP8X4 = mybir.dt.float8_e4m3fn_x4
ACT = mybir.ActivationFunctionType
ALU = mybir.AluOpType

P = 128
PACK = 4
T = 2048
S = 512
HALF = 256
QUARTER = 128
FLOPS = 2 * 2 * 512 * 512 * 512


def tile_picked_absgate_none_p_kernel(
    tc, x_words, x_scales, w1, gn, w2, offs, n1, n2, n3, out
):
    nc = tc.nc
    with ExitStack() as ctx:
        keep = ctx.enter_context(tc.tile_pool(name="keep", bufs=1))
        psum = ctx.enter_context(tc.psum_pool(name="psum", bufs=1))

        def sb(name, shape, dtype, tag=""):
            return keep.tile(shape, dtype, name=name, tag=tag or name, align_bytes=64)

        def entries(lst, start, width):
            return lst[:, start // 16 : (start + width) // 16]

        offs_sb = keep.tile([P, S // 16], U16, name="offs_sb")
        n1_sb = keep.tile([P, S // 16], U16, name="n1_sb")
        n2_sb = keep.tile([P, S // 16], U16, name="n2_sb")
        n3_sb = keep.tile([P, S // 16], U16, name="n3_sb")

        xs_all = sb("xs_all", [P, T], U8)
        nc.vector.memset(xs_all[:].bitcast(I32), 0)
        for q in range(4):
            nc.scalar.dma_start(
                out=xs_all[32 * q : 32 * q + 4, :].bitcast(I32), in_=x_scales[0][4 * q : 4 * q + 4, :].bitcast(I32)
            )
        warm = sb("warm", [P, 8], F32)
        nc.vector.memset(warm[:, 0:1], 0.0)
        nc.scalar.activation(warm[:, 4:5], warm[:, 0:1], ACT.Sigmoid)

        nc.sync.dma_start(offs_sb[:], offs)
        nc.sync.dma_start(n1_sb[:], n1)
        nc.sync.dma_start(n2_sb[:], n2)
        w1_rows = w1.rearrange("(p j) c -> p j c", j=PACK)
        w1_raw = []
        for a in range(2):
            raw = sb("w1_raw%d" % a, [P, PACK, HALF], F32, tag="chain_a" if a == 0 else "")
            nc.sync.dma_start(out=raw[:], in_=w1_rows[:, :, a * HALF : (a + 1) * HALF])
            w1_raw.append(raw)
        xw_all = sb("xw_all", [P, T], I32)
        nc.sync.dma_start(out=xw_all[:], in_=x_words[0].rearrange("p n t -> p (n t)").bitcast(I32))
        nc.sync.dma_start(n3_sb[:], n3)
        gain = sb("gain", [P, PACK], F32)
        nc.gpsimd.dma_start(out=gain[:], in_=gn.rearrange("(p j) o -> p (j o)", j=PACK))

        g1 = sb("g1", [P, PACK * S], BF16)
        g1_v = g1[:].rearrange("p (t m j) -> p m t j", t=PACK, j=PACK)
        for a in range(2):
            nc.vector.tensor_copy(g1_v[:, 64 * a : 64 * (a + 1)], w1_raw[a][:].rearrange("p j (m t) -> p m t j", t=PACK))
        w2_raw = sb("w2_raw", [P, PACK, S], F32, tag="chain_a")
        nc.sync.dma_start(out=w2_raw[:], in_=w2.rearrange("(p j) c -> p j c", j=PACK))
        xs = sb("xs", [P, S], U8)
        xw = sb("xw", [P, S], U32)
        nc.vector.tensor_copy(xs[:], xs_all[:].indirect(offs_sb[:]))
        w1c = sb("w1c", [P, S], U32)
        w1s = sb("w1s", [P, S], U8)
        nc.vector.quantize_mx(out=w1c[:].bitcast(FP8X4), scales=w1s[:], in_=g1[:])
        for a in range(2):
            nc.vector.tensor_copy(
                xw[:, a * HALF : (a + 1) * HALF], xw_all[:].bitcast(U32).indirect(entries(offs_sb, a * HALF, HALF))
            )

        sign = sb("sign", [P, PACK], F32)
        nc.scalar.activation(sign[:], gain[:], ACT.Sign)

        def product(acc, wc, ws, t, rc, rs):
            nc.tensor.matmul_mx(
                out=acc,
                lhsT=wc[:, t * P : (t + 1) * P].bitcast(FP8X4),
                lhsT_scale=ws[:, t * P : (t + 1) * P],
                rhs=rc.bitcast(FP8X4),
                rhs_scale=rs,
                start=True,
                stop=True,
            )

        y_win = [sb("y_win%d" % t, [P, S], F32) for t in range(PACK)]
        d0 = sb("d0", [P, PACK * HALF], F32)
        y_lo_even = [sb("y_lo%d" % t, [P, HALF], F32) for t in (0, 2)]
        y_lo = [y_lo_even[0][:], d0[:, 0:HALF], y_lo_even[1][:], d0[:, 2 * HALF : 3 * HALF]]
        y_hi = [sb("y_hi%d" % t, [P, HALF], F32) for t in range(PACK)]
        lo_acc = [psum.tile([P, HALF], F32, name="acc_lo%d" % t, tag="b%d" % t) for t in range(2)]
        hi_acc = [psum.tile([P, HALF], F32, name="acc_hi%d" % t, tag="b%d" % (4 + t)) for t in range(2)]
        full_acc = [psum.tile([P, S], F32, name="acc_y%d" % t, tag="b%d" % t) for t in (2, 3)]
        for t in range(2):
            product(lo_acc[t][:], w1c, w1s, t, xw[:, 0:HALF], xs[:, 0:HALF])
        for t in range(2):
            product(hi_acc[t][:], w1c, w1s, t, xw[:, HALF:S], xs[:, HALF:S])
        for t in (2, 3):
            product(full_acc[t - 2][:], w1c, w1s, t, xw[:], xs[:])

        def scaled(dst, acc, t):
            nc.scalar.activation(dst, acc, ACT.Copy, scale=gain[:, t : t + 1])

        for t in range(2):
            scaled(y_win[t][:, 0:HALF], lo_acc[t][:], t)
            scaled(y_lo[t], lo_acc[t][:], t)
        nc.vector.tensor_scalar(y_win[0][:, HALF:S], hi_acc[0][:], gain[:, 0:1], None, ALU.mult)
        scaled(y_win[1][:, HALF:S], hi_acc[1][:], 1)
        for t in (2, 3):
            scaled(y_win[t][:], full_acc[t - 2][:], t)
            scaled(y_lo[t], full_acc[t - 2][:, 0:HALF], t)
        for t in range(PACK):
            nc.sync.dma_start(out=y_hi[t][:], in_=y_win[t][:, HALF:S])

        def first(t, start, plain):
            part = sb("part%d_%d" % (start, t), [P, HALF], F32)
            nc.vector.tensor_tensor(part[:], y_win[t][:].indirect(entries(n1_sb, start, HALF)), plain, ALU.subtract)
            return part

        def second(t, start, width, part, d):
            nc.vector.tensor_tensor(
                d[:, t * width : (t + 1) * width], y_win[t][:].indirect(entries(n2_sb, start, width)), part, ALU.add
            )

        def magnitude(zb, d):
            nc.scalar.activation(
                zb[:].rearrange("p (c i t) -> p c t i", i=4, t=PACK),
                d[:].rearrange("p (t c i) -> p c t i", i=4, t=PACK),
                ACT.Abs,
            )

        def quantise(name, zb, width):
            zc = sb("zc" + name, [P, width], U32)
            zs = sb("zs" + name, [P, width], U8)
            nc.vector.quantize_mx(out=zc[:].bitcast(FP8X4), scales=zs[:], in_=zb[:])
            return zc, zs

        for pair in ((0, 1), (2, 3)):
            parts = [first(t, 0, y_lo[t]) for t in pair]
            for t, part in zip(pair, parts):
                second(t, 0, HALF, part[:], d0)
        pairs = sb("pairs", [P, PACK * S], BF16)
        pairs_v = pairs[:].rearrange("p (u c e) -> p u c e", u=2, e=2)
        for j in range(PACK):
            nc.scalar.activation(pairs_v[:, j // 2, :, j % 2], w2_raw[:, j, :], ACT.Copy, scale=sign[:, j : j + 1])
        zb0 = sb("zb0", [P, PACK * HALF], BF16, tag="chain_a")
        magnitude(zb0, d0)
        hi_parts = [first(t, HALF, y_hi[t][:]) for t in range(PACK)]
        g2 = sb("g2", [P, PACK * S], BF16, tag="chain_b")
        nc.scalar.copy(
            g2[:].bitcast(F32).rearrange("p (t m u) -> p m t u", t=PACK, u=2),
            pairs[:].bitcast(F32).rearrange("p (u m t) -> p m t u", t=PACK, u=2),
        )
        zq0 = quantise("0", zb0, HALF)
        d1 = sb("d1", [P, PACK * QUARTER], F32, tag="chain_a")
        for t in range(PACK):
            second(t, HALF, QUARTER, hi_parts[t][:, 0:QUARTER], d1)
        zb1 = sb("zb1", [P, PACK * QUARTER], BF16)
        magnitude(zb1, d1)
        w2c = sb("w2c", [P, S], U32)
        w2s = sb("w2s", [P, S], U8)
        nc.vector.quantize_mx(out=w2c[:].bitcast(FP8X4), scales=w2s[:], in_=g2[:])

        h_win = [sb("h_win%d" % t, [P, S], F32) for t in range(PACK)]
        h_half = [[sb("h_half%d_%d" % (a, t), [P, HALF], F32) for t in range(PACK)] for a in range(2)]
        lo_h = [psum.tile([P, HALF], F32, name="acc_h0_%d" % t, tag="b%d" % t) for t in range(PACK)]
        for t in range(PACK):
            product(lo_h[t][:], w2c, w2s, t, zq0[0][:], zq0[1][:])

        def keep_half(a, t, acc, copy):
            copy(h_win[t][:, a * HALF : (a + 1) * HALF], acc)
            nc.sync.dma_start(out=h_half[a][t][:], in_=h_win[t][:, a * HALF : (a + 1) * HALF])

        for t in range(2):
            keep_half(0, t, lo_h[t][:], nc.scalar.copy)
        d2 = sb("d2", [P, PACK * QUARTER], F32, tag="chain_b")
        zb2 = sb("zb2", [P, PACK * QUARTER], BF16)
        for t in range(PACK):
            second(t, HALF + QUARTER, QUARTER, hi_parts[t][:, QUARTER:HALF], d2)
            if t % 2 == 1:
                nc.scalar.activation(
                    zb2[:].rearrange("p (c i u e) -> p u c e i", i=4, u=2, e=2)[:, t // 2],
                    d2[:].rearrange("p (u e c i) -> p u c e i", i=4, u=2, e=2)[:, t // 2],
                    ACT.Abs,
                )
        zq1 = quantise("1", zb1, QUARTER)
        hi_h = [psum.tile([P, 2, QUARTER], F32, name="acc_h1_%d" % t, tag="b%d" % (4 + t)) for t in range(PACK)]
        for t in range(PACK):
            product(hi_h[t][:, 0, :], w2c, w2s, t, zq1[0][:], zq1[1][:])
        keep_half(0, 2, lo_h[2][:], nc.vector.tensor_copy)
        keep_half(0, 3, lo_h[3][:], nc.scalar.copy)
        zq2 = quantise("2", zb2, QUARTER)
        for t in range(PACK):
            product(hi_h[t][:, 1, :], w2c, w2s, t, zq2[0][:], zq2[1][:])

        out_rows = out.rearrange("(p t) c -> p t c", t=PACK)
        diff = [sb("diff%d" % a, [P, PACK * HALF], F32) for a in range(2)]
        gate = [sb("gate%d" % a, [P, PACK * HALF], F32) for a in range(2)]
        res = [sb("res%d" % a, [P, PACK * HALF], F32) for a in range(2)]

        def look_up(a, t, lo, width):
            places = entries(n3_sb, a * HALF + lo, width)
            cols = slice(t * HALF + lo, t * HALF + lo + width)
            nc.vector.tensor_tensor(
                diff[a][:, cols], h_win[t][:].indirect(places), h_half[a][t][:, lo : lo + width], ALU.subtract
            )
            nc.scalar.activation(gate[a][:, cols], h_win[t][:].indirect(places), ACT.Sigmoid)

        def finish(a, t, tiles, lo, width, queue):
            cols = slice(t * HALF + lo, (t + tiles - 1) * HALF + lo + width)
            nc.vector.scalar_tensor_tensor(res[a][:, cols], diff[a][:, cols], -1.0, gate[a][:, cols], ALU.mult, ALU.mult)
            queue.dma_start(
                out=out_rows[:, t : t + tiles, a * HALF + lo : a * HALF + lo + width],
                in_=res[a][:, cols].rearrange("p (t c) -> p t c", t=tiles),
            )

        def upper(t):
            keep_half(1, t, hi_h[t][:].rearrange("p a c -> p (a c)"), nc.scalar.copy)

        upper(0)
        upper(1)
        look_up(0, 0, 0, HALF)
        upper(2)
        look_up(0, 1, 0, HALF)
        upper(3)
        look_up(0, 2, 0, HALF)
        finish(0, 0, 2, 0, HALF, nc.sync)
        look_up(0, 3, 0, HALF)
        look_up(1, 0, 0, HALF)
        finish(0, 2, 2, 0, HALF, nc.sync)
        look_up(1, 1, 0, HALF)
        look_up(1, 2, 0, HALF)
        finish(1, 0, 2, 0, HALF, nc.sync)
        look_up(1, 3, 0, HALF)
        finish(1, 2, 1, 0, HALF, nc.sync)
        finish(1, 3, 1, 0, HALF, nc.sync)
